import numpy as np
import ml_dtypes


def mxq(x, axis, fmt="e4m3"):
    dtype, down = {"e4m3": (ml_dtypes.float8_e4m3fn, 7), "e5m2": (ml_dtypes.float8_e5m2, 14)}[fmt]
    v = np.moveaxis(np.asarray(x, np.float32).astype(ml_dtypes.bfloat16).astype(np.float64), axis, -1)
    blocks = v.reshape(v.shape[:-1] + (-1, 32))
    amax = np.abs(blocks).max(-1, keepdims=True)
    byte = np.maximum(np.where(amax > 0, np.frexp(amax)[1] - 1 + 127, 0) - down, 1)
    scale = np.exp2(byte - 127.0)
    codes = (blocks / scale).astype(np.float32).astype(dtype).astype(np.float64)
    return np.moveaxis((codes * scale).reshape(v.shape), -1, axis)


WIDE = False


def mx_kscale(k):
    if not WIDE:
        return np.ones(k)
    levels = np.array([18, -18])
    if k % 512:
        return np.exp2(np.random.permutation(np.resize(levels, k // 32))).repeat(32)
    a = np.empty((k // 512, 16))
    for p in range(k // 512):
        a[p, :8] = np.random.permutation(np.resize(levels, 8))
        for g in range(8):
            far = levels[np.abs(levels - a[p, g]) >= 10]
            a[p, g + 8] = far[np.random.randint(len(far))]
    return np.exp2(a.ravel()).repeat(32)


def f64(x):
    return np.asarray(x).astype(np.float64)


def striped(idx):
    return np.tile(np.asarray(idx).reshape(-1, 16).T, (8, 1)).astype(np.uint16)


def unstriped(offs):
    return offs[:16].T.reshape(-1).astype(np.int64)


B, N, T, D, R = 2, 512, 2048, 512, 512


def setup_inputs():
    n = np.random.standard_normal
    idx = np.random.permutation(T)[:B * N]
    u = np.ones(T)
    u[idx] = mx_kscale(B * N)
    us = u[idx].reshape(B, N)
    z = mx_kscale(R)[:, None]
    act = n((B, R, N))
    return {
        "zT": (act.transpose(0, 2, 1) * us[:, :, None]).astype(np.float32),
        "wT": (n((D, T)) / np.sqrt(N) / u).astype(np.float32),
        "xm": (n((B, R, D))).astype(np.float32),
        "wt": (np.random.uniform(0.5, 1.5, (B, R, 1)) / np.sqrt(R) * z).astype(np.float32),
        "zm": (act / z).astype(np.float32),
        "offs": striped(idx),
    }


def reference(zT, wT, xm, wt, zm, offs):
    idx = unstriped(offs)
    pick = lambda x: x[:, idx].reshape(x.shape[0], B, N).transpose(1, 0, 2)
    rec = mxq(f64(zT), 1, "e4m3").transpose(0, 2, 1) @ mxq(pick(f64(wT)), 2, "e4m3").transpose(0, 2, 1)
    q = rec - f64(xm)
    e = f64(wt) * np.minimum(np.maximum(q, -1.0), 1.0)
    dw = mxq(e, 1, "e5m2").transpose(0, 2, 1) @ mxq(f64(zm), 1, "e4m3")
    gw = np.zeros((D, T))
    gw[:, idx] = dw.transpose(1, 0, 2).reshape(D, B * N)
    return gw

@@ -1,0 +1,275 @@
+from contextlib import ExitStack
+
+import concourse.mybir as mybir
+from concourse.masks import make_identity
+
+B, N, T, D, R = 2, 512, 2048, 512, 512
+FLOPS = 2 * 2 * B * N * D * R
+
+F32 = mybir.dt.float32
+BF16 = mybir.dt.bfloat16
+U32 = mybir.dt.uint32
+U16 = mybir.dt.uint16
+U8 = mybir.dt.uint8
+E4M3 = mybir.dt.float8_e4m3fn_x4
+E5M2 = mybir.dt.float8_e5m2_x4
+ALU = mybir.AluOpType
+COPY = mybir.ActivationFunctionType.Copy
+
+P = 128
+PACK = 4
+HALF = 256
+COLS = N // 16
+
+
+def tile_attend_gdi_hub_w_kernel(tc, zT, wT, xm, wt, zm, offs, out):
+    nc = tc.nc
+    with ExitStack() as ctx:
+        keep = ctx.enter_context(tc.tile_pool(name="keep", bufs=1))
+        work = ctx.enter_context(tc.tile_pool(name="work", bufs=2))
+        turn_psum = ctx.enter_context(tc.psum_pool(name="turn_psum", bufs=2))
+        rec_psum = ctx.enter_context(tc.psum_pool(name="rec_psum", bufs=3))
+        grad_psum = ctx.enter_context(tc.psum_pool(name="grad_psum", bufs=3))
+
+        offsets = keep.tile([P, B * COLS], U16, name="offsets")
+        nc.sync.dma_start(offsets[:], offs)
+
+        table = {}
+        zT_raw = {}
+        zm_raw = {}
+        target = {}
+
+        def load_table(c):
+            table[c] = keep.tile([P, T], F32, name="table%d" % c, tag=("grad3" if c == 3 else "table%d" % c), align_bytes=64)
+            nc.sync.dma_start(table[c][:], wT[c * P : (c + 1) * P, :])
+
+        def load_rows(src, raw, name, b):
+            for h in range(2):
+                raw[b, h] = keep.tile([P, PACK, HALF], F32, name="%s%d%d" % (name, b, h), tag="%s%d%d" % (name, b, h), align_bytes=64)
+                nc.sync.dma_start(
+                    raw[b, h][:], src[b].rearrange("(p j) w -> p j w", j=PACK)[:, :, h * HALF : (h + 1) * HALF]
+                )
+
+        def load_target(b, c0, c1):
+            t = keep.tile([P, PACK, (c1 - c0) * P], F32, name="target%d%d" % (b, c0), tag="target%d%d" % (b, c0), align_bytes=64)
+            nc.sync.dma_start(t[:], xm[b].rearrange("(p t) d -> p t d", t=PACK)[:, :, c0 * P : c1 * P])
+            for c in range(c0, c1):
+                target[c, b] = t[:, :, (c - c0) * P : (c - c0 + 1) * P]
+
+        load_table(0)
+        load_rows(zT, zT_raw, "zT_raw", 0)
+        weight = keep.tile([P, B, PACK], F32, name="weight")
+        nc.sync.dma_start(weight[:], wt.rearrange("b (p t) o -> p b (t o)", t=PACK))
+        load_target(0, 0, 1)
+        load_rows(zm, zm_raw, "zm_raw", 0)
+        load_table(1)
+        load_target(0, 1, 2)
+        load_rows(zT, zT_raw, "zT_raw", 1)
+        load_target(1, 0, 1)
+        load_rows(zm, zm_raw, "zm_raw", 1)
+        load_table(2)
+        load_target(1, 1, 2)
+        load_target(0, 2, 3)
+        load_table(3)
+        load_target(1, 2, 3)
+        load_target(0, 3, 4)
+        load_target(1, 3, 4)
+
+        identity = keep.tile([P, P], F32, name="identity")
+        make_identity(nc, identity[:])
+
+        window = []
+        for c in range(3):
+            w = keep.tile([P, T], F32, name="window%d" % c)
+            (nc.vector if c < 2 else nc.gpsimd).memset(w[:], 0.0)
+            window.append(w)
+
+        def cast(engine, out_ap, in_ap):
+            if engine == "vector":
+                nc.vector.tensor_copy(out_ap, in_ap)
+            else:
+                nc.scalar.activation(out_ap, in_ap, COPY)
+
+        def quantize(name, grouped, words, fmt):
+            codes = keep.tile([P, words], U32, name=name + "_codes", tag=name + "_codes", align_bytes=64)
+            scales = keep.tile([P, words], U8, name=name + "_scales", align_bytes=64)
+            nc.vector.quantize_mx(out=codes[:].bitcast(fmt), scales=scales[:], in_=grouped)
+            return codes, scales
+
+        zT_q = {}
+        zm_q = {}
+
+        def prepare_zT(b, engines):
+            grouped = keep.tile([P, R * PACK], BF16, name="zT_grouped%d" % b, tag=["zT_grouped", "e_first0"][b], align_bytes=64)
+            view = grouped[:].rearrange("p (t m j) -> p m j t", t=PACK, j=PACK)
+            for h in range(2):
+                cast(engines[h], view[:, h * 64 : (h + 1) * 64], zT_raw[b, h][:].rearrange("p j (m t) -> p m j t", t=PACK))
+            zT_q[b] = quantize("zT%d" % b, grouped[:], R, E4M3)
+
+        def prepare_zm(b, engines):
+            grouped = keep.tile([P, N * PACK], BF16, name="zm_grouped%d" % b, tag=["picked2", "zT_raw11"][b], align_bytes=64)
+            view = grouped[:].rearrange("p (c i j) -> p c j i", i=4, j=PACK)
+            for h in range(2):
+                cast(engines[h], view[:, h * 64 : (h + 1) * 64], zm_raw[b, h][:].rearrange("p j (c i) -> p c j i", i=4))
+            zm_q[b] = quantize("zm%d" % b, grouped[:], N, E4M3)
+
+        units = [(0, 0), (1, 0), (0, 1), (1, 1), (2, 0), (2, 1), (3, 0), (3, 1)]
+        table16 = {}
+        picked = {}
+        atoms_q = {}
+        clipped = {}
+        e_q = {}
+        e_grouped = {}
+        residual = {}
+        banks = {}
+
+        def listed(tile, b, lo=0, hi=COLS):
+            return tile[:].indirect(offsets[:, b * COLS + lo : b * COLS + hi])
+
+        def cast_table(c, h):
+            if c not in table16:
+                table16[c] = keep.tile([P, T], BF16, name="table16_%d" % c, tag=("target11" if c == 3 else "zm_raw11"), align_bytes=64)
+            cols = slice(h * T // 2, (h + 1) * T // 2)
+            nc.scalar.activation(table16[c][:, cols], table[c][:, cols], COPY)
+
+        def gather(k):
+            c, b = units[k]
+            picked[k] = keep.tile([P, N], BF16, name="picked%d" % k, tag=("e%d_codes" % (k - 3) if k >= 5 else ["picked0", "e_first0", "picked2", "e0_codes", "e1_codes"][k]), align_bytes=64)
+            if k < 5:
+                nc.vector.tensor_copy(picked[k][:], listed(table[c], b))
+            else:
+                nc.scalar.activation(picked[k][:], listed(table16[c], b), COPY)
+
+        def turn(k):
+            words = picked[k][:].bitcast(F32)
+            turned = turn_psum.tile([P, 2, P], F32, name="turned")
+            for u in range(2):
+                nc.tensor.transpose(turned[:, u, :], words[:, u : 2 * P : 2], identity[:])
+            grouped = keep.tile([P, P * PACK], BF16, name="atoms_grouped%d" % k, tag=("grad%d" % (k - 3) if k >= 4 else ["zT_raw00", "e0_codes", "atoms2", "zm_raw10"][k]), align_bytes=64)
+            nc.scalar.copy(
+                grouped[:].bitcast(F32).rearrange("p (d u) -> p d u", u=2), turned[:].rearrange("p u d -> p d u")
+            )
+            atoms_q[k] = quantize("atoms%d" % k, grouped[:], P, E4M3)
+
+        def rebuild(k):
+            c, b = units[k]
+            rec = rec_psum.tile([P, PACK, P], F32, name="rec")
+            z_codes, z_scales = zT_q[b]
+            a_codes, a_scales = atoms_q[k]
+            for t in range(PACK):
+                nc.tensor.matmul_mx(
+                    out=rec[:, t, :],
+                    lhsT=z_codes[:, t * P : (t + 1) * P].bitcast(E4M3),
+                    lhsT_scale=z_scales[:, t * P : (t + 1) * P],
+                    rhs=a_codes[:].bitcast(E4M3),
+                    rhs_scale=a_scales[:],
+                    start=True,
+                    stop=True,
+                )
+            residual[k] = keep.tile([P, PACK, P], F32, name="residual%d" % k, tag="chain%d" % (k - 1), align_bytes=64)
+            nc.vector.tensor_tensor(residual[k][:], rec[:], target[c, b], ALU.subtract)
+
+        def clip(k):
+            clipped[k] = keep.tile([P, P, PACK], F32, name="clipped%d" % k, tag="chain%d" % k, align_bytes=64)
+            nc.vector.tensor_scalar(
+                clipped[k][:].rearrange("p (c i) t -> p c t i", i=4),
+                residual[k][:].rearrange("p t (c i) -> p c t i", i=4),
+                -1.0,
+                1.0,
+                ALU.max,
+                ALU.min,
+            )
+
+        def weigh(k):
+            c, b = units[k]
+            grouped = keep.tile([P, P * PACK], BF16, name="e_grouped%d" % k, tag=("grad%d" % (k - 2) if k >= 2 else "e_first%d" % k), align_bytes=64)
+            (nc.vector if k == 0 else nc.gpsimd).tensor_tensor(
+                grouped[:].rearrange("p (d t) -> p d t", t=PACK),
+                clipped[k][:],
+                weight[:, b : b + 1, :].to_broadcast([P, P, PACK]),
+                ALU.mult,
+            )
+            e_grouped[k] = grouped
+
+        def differentiate(k):
+            c, b = units[k]
+            e_q[k] = quantize("e%d" % k, e_grouped[k][:], P, E5M2)
+            banks[k] = grad_psum.tile([P, N], F32, name="grad_bank")
+            nc.tensor.matmul_mx(
+                out=banks[k][:],
+                lhsT=e_q[k][0][:].bitcast(E5M2),
+                lhsT_scale=e_q[k][1][:],
+                rhs=zm_q[b][0][:].bitcast(E4M3),
+                rhs_scale=zm_q[b][1][:],
+                start=True,
+                stop=True,
+            )
+
+        def scatter(k, h):
+            c, b = units[k]
+            tag = "grad%d" % k
+            if h == 1 and k == 0:
+                tag = "target01"
+            elif h == 1 and k + 2 < len(units):
+                tag = "target%d%d" % (units[k + 2][1], units[k + 2][0])
+            elif h == 1 and k + 1 < len(units):
+                tag = "chain%d" % (k + 1)
+            elif h == 1:
+                tag = "last"
+            part = keep.tile([P, HALF], F32, name="grad%d%d" % (k, h), tag=tag, align_bytes=64)
+            if (k, h) == (0, 1):
+                nc.vector.tensor_copy(part[:], banks[k][:, h * HALF : (h + 1) * HALF])
+            else:
+                nc.scalar.copy(part[:], banks[k][:, h * HALF : (h + 1) * HALF])
+            nc.vector.tensor_copy(listed(window[c % 3], b, h * COLS // 2, (h + 1) * COLS // 2), part[:])
+            if b == B - 1 and h == 1:
+                nc.sync.dma_start(out[c * P : (c + 1) * P, :], window[c % 3][:])
+
+        gather(0)
+        prepare_zT(0, ("scalar", "vector"))
+        turn(0)
+        rebuild(0)
+        gather(2)
+        turn(2)
+        clip(0)
+        prepare_zm(0, ("scalar", "scalar"))
+        weigh(0)
+        differentiate(0)
+        gather(1)
+        scatter(0, 0)
+        turn(1)
+        gather(3)
+        rebuild(1)
+        clip(1)
+        scatter(0, 1)
+        prepare_zT(1, ("scalar", "scalar"))
+        weigh(1)
+        rebuild(2)
+        differentiate(1)
+        clip(2)
+        prepare_zm(1, ("scalar", "scalar"))
+        turn(3)
+        gather(4)
+        cast_table(2, 0)
+        scatter(1, 0)
+        cast_table(2, 1)
+        for k in range(1, len(units)):
+            if k + 3 < len(units):
+                turn(k + 3)
+            if k + 1 < len(units):
+                weigh(k + 1)
+            if k + 2 < len(units):
+                rebuild(k + 2)
+            if k + 1 < len(units):
+                differentiate(k + 1)
+            if k + 2 < len(units):
+                clip(k + 2)
+            scatter(k, 1)
+            if k == 2:
+                cast_table(3, 1)
+            if k + 1 < len(units):
+                scatter(k + 1, 0)
+            if k + 4 < len(units):
+                gather(k + 4)
+            if k == 1:
+                cast_table(3, 0)

@@ -40,7 +40,7 @@ def tile_attend_gdi_hub_w_kernel(tc, zT, wT, xm, wt, zm, offs, out):
         target = {}
 
         def load_table(c):
-            table[c] = keep.tile([P, T], F32, name="table%d" % c, tag=("grad3" if c == 3 else "table%d" % c), align_bytes=64)
+            table[c] = keep.tile([P, T], F32, name="table%d" % c, tag="table%d" % c, align_bytes=64)
             nc.sync.dma_start(table[c][:], wT[c * P : (c + 1) * P, :])
 
         def load_rows(src, raw, name, b):
@@ -128,14 +128,13 @@ def tile_attend_gdi_hub_w_kernel(tc, zT, wT, xm, wt, zm, offs, out):
 
         def cast_table(c, h):
             if c not in table16:
-                table16[c] = keep.tile([P, T], BF16, name="table16_%d" % c, tag=("target11" if c == 3 else "zm_raw11"), align_bytes=64)
-            cols = slice(h * T // 2, (h + 1) * T // 2)
-            nc.scalar.activation(table16[c][:, cols], table[c][:, cols], COPY)
+                table16[c] = keep.tile([P, T], BF16, name="table16_%d" % c, tag="table2", align_bytes=64)
+            nc.scalar.activation(table16[c][:], table[c][:], COPY)
 
         def gather(k):
             c, b = units[k]
-            picked[k] = keep.tile([P, N], BF16, name="picked%d" % k, tag=("e%d_codes" % (k - 3) if k >= 5 else ["picked0", "e_first0", "picked2", "e0_codes", "e1_codes"][k]), align_bytes=64)
-            if k < 5:
+            picked[k] = keep.tile([P, N], BF16, name="picked%d" % k, tag=("e%d_codes" % (k - 4) if k >= 5 else ["picked0", "e_first0", "picked2", "e0_codes", "e_first0"][k]), align_bytes=64)
+            if k < 6:
                 nc.vector.tensor_copy(picked[k][:], listed(table[c], b))
             else:
                 nc.scalar.activation(picked[k][:], listed(table16[c], b), COPY)
@@ -145,7 +144,7 @@ def tile_attend_gdi_hub_w_kernel(tc, zT, wT, xm, wt, zm, offs, out):
             turned = turn_psum.tile([P, 2, P], F32, name="turned")
             for u in range(2):
                 nc.tensor.transpose(turned[:, u, :], words[:, u : 2 * P : 2], identity[:])
-            grouped = keep.tile([P, P * PACK], BF16, name="atoms_grouped%d" % k, tag=("grad%d" % (k - 3) if k >= 4 else ["zT_raw00", "e0_codes", "atoms2", "zm_raw10"][k]), align_bytes=64)
+            grouped = keep.tile([P, P * PACK], BF16, name="atoms_grouped%d" % k, tag=("grad%d" % (k - 4) if k >= 5 else ["zT_raw00", "e0_codes", "atoms2", "zm_raw10", "zm_raw11"][k]), align_bytes=64)
             nc.scalar.copy(
                 grouped[:].bitcast(F32).rearrange("p (d u) -> p d u", u=2), turned[:].rearrange("p u d -> p d u")
             )
@@ -166,8 +165,14 @@ def tile_attend_gdi_hub_w_kernel(tc, zT, wT, xm, wt, zm, offs, out):
                     start=True,
                     stop=True,
                 )
-            residual[k] = keep.tile([P, PACK, P], F32, name="residual%d" % k, tag="chain%d" % (k - 1), align_bytes=64)
-            nc.vector.tensor_tensor(residual[k][:], rec[:], target[c, b], ALU.subtract)
+            if k < 3:
+                residual[k] = keep.tile([P, PACK, P], F32, name="residual%d" % k, tag="chain%d" % (k - 1), align_bytes=64)
+                nc.vector.tensor_tensor(residual[k][:], rec[:], target[c, b], ALU.subtract)
+            else:
+                staged = keep.tile([P, PACK, P], F32, name="staged%d" % k, tag="grad%d" % (k - 1), align_bytes=64)
+                nc.scalar.copy(staged[:], rec[:])
+                residual[k] = keep.tile([P, PACK, P], F32, name="residual%d" % k, tag="chain%d" % (k - 1), align_bytes=64)
+                nc.gpsimd.tensor_tensor(residual[k][:], staged[:], target[c, b], ALU.subtract)
 
         def clip(k):
             clipped[k] = keep.tile([P, P, PACK], F32, name="clipped%d" % k, tag="chain%d" % k, align_bytes=64)
@@ -247,29 +252,28 @@ def tile_attend_gdi_hub_w_kernel(tc, zT, wT, xm, wt, zm, offs, out):
         rebuild(2)
         differentiate(1)
         clip(2)
+        gather(4)
         prepare_zm(1, ("scalar", "scalar"))
         turn(3)
-        gather(4)
-        cast_table(2, 0)
+        turn(4)
+        gather(5)
         scatter(1, 0)
-        cast_table(2, 1)
+        weigh(2)
+        rebuild(3)
+        cast_table(3, 0)
         for k in range(1, len(units)):
-            if k + 3 < len(units):
-                turn(k + 3)
-            if k + 1 < len(units):
-                weigh(k + 1)
-            if k + 2 < len(units):
-                rebuild(k + 2)
             if k + 1 < len(units):
                 differentiate(k + 1)
+            if k + 4 < len(units):
+                turn(k + 4)
             if k + 2 < len(units):
                 clip(k + 2)
             scatter(k, 1)
-            if k == 2:
-                cast_table(3, 1)
             if k + 1 < len(units):
                 scatter(k + 1, 0)
-            if k + 4 < len(units):
-                gather(k + 4)
-            if k == 1:
-                cast_table(3, 0)
+            if k + 2 < len(units):
+                weigh(k + 2)
+            if k + 3 < len(units):
+                rebuild(k + 3)
+            if k + 5 < len(units):
+                gather(k + 5)

@@ -20,6 +20,7 @@ P = 128
 PACK = 4
 HALF = 256
 COLS = N // 16
+EARLY = 3
 
 
 def tile_attend_gdi_hub_w_kernel(tc, zT, wT, xm, wt, zm, offs, out):
@@ -32,7 +33,6 @@ def tile_attend_gdi_hub_w_kernel(tc, zT, wT, xm, wt, zm, offs, out):
         grad_psum = ctx.enter_context(tc.psum_pool(name="grad_psum", bufs=3))
 
         offsets = keep.tile([P, B * COLS], U16, name="offsets")
-        nc.sync.dma_start(offsets[:], offs)
 
         table = {}
         zT_raw = {}
@@ -57,6 +57,7 @@ def tile_attend_gdi_hub_w_kernel(tc, zT, wT, xm, wt, zm, offs, out):
                 target[c, b] = t[:, :, (c - c0) * P : (c - c0 + 1) * P]
 
         load_table(0)
+        nc.sync.dma_start(offsets[:], offs)
         load_rows(zT, zT_raw, "zT_raw", 0)
         weight = keep.tile([P, B, PACK], F32, name="weight")
         nc.sync.dma_start(weight[:], wt.rearrange("b (p t) o -> p b (t o)", t=PACK))
@@ -126,15 +127,16 @@ def tile_attend_gdi_hub_w_kernel(tc, zT, wT, xm, wt, zm, offs, out):
         def listed(tile, b, lo=0, hi=COLS):
             return tile[:].indirect(offsets[:, b * COLS + lo : b * COLS + hi])
 
-        def cast_table(c, h):
+        def cast_table(c, h, engine):
             if c not in table16:
-                table16[c] = keep.tile([P, T], BF16, name="table16_%d" % c, tag="table2", align_bytes=64)
-            nc.scalar.activation(table16[c][:], table[c][:], COPY)
+                table16[c] = keep.tile([P, T], BF16, name="table16_%d" % c, tag=("picked4" if c == 3 else "zm_raw11"), align_bytes=64)
+            cols = slice(h * T // 2, (h + 1) * T // 2)
+            cast(engine, table16[c][:, cols], table[c][:, cols])
 
         def gather(k):
             c, b = units[k]
-            picked[k] = keep.tile([P, N], BF16, name="picked%d" % k, tag=("e%d_codes" % (k - 4) if k >= 5 else ["picked0", "e_first0", "picked2", "e0_codes", "e_first0"][k]), align_bytes=64)
-            if k < 6:
+            picked[k] = keep.tile([P, N], BF16, name="picked%d" % k, tag=("clipped%d" % (k - 2) if k >= 5 else ["picked0", "e_first0", "picked2", "e0_codes", "picked4"][k]), align_bytes=64)
+            if c < 2:
                 nc.vector.tensor_copy(picked[k][:], listed(table[c], b))
             else:
                 nc.scalar.activation(picked[k][:], listed(table16[c], b), COPY)
@@ -144,7 +146,7 @@ def tile_attend_gdi_hub_w_kernel(tc, zT, wT, xm, wt, zm, offs, out):
             turned = turn_psum.tile([P, 2, P], F32, name="turned")
             for u in range(2):
                 nc.tensor.transpose(turned[:, u, :], words[:, u : 2 * P : 2], identity[:])
-            grouped = keep.tile([P, P * PACK], BF16, name="atoms_grouped%d" % k, tag=("grad%d" % (k - 4) if k >= 5 else ["zT_raw00", "e0_codes", "atoms2", "zm_raw10", "zm_raw11"][k]), align_bytes=64)
+            grouped = keep.tile([P, P * PACK], BF16, name="atoms_grouped%d" % k, tag=("atoms%d" % k if k >= 4 else ["zT_raw00", "e0_codes", "atoms2", "zm_raw10"][k]), align_bytes=64)
             nc.scalar.copy(
                 grouped[:].bitcast(F32).rearrange("p (d u) -> p d u", u=2), turned[:].rearrange("p u d -> p d u")
             )
@@ -165,35 +167,42 @@ def tile_attend_gdi_hub_w_kernel(tc, zT, wT, xm, wt, zm, offs, out):
                     start=True,
                     stop=True,
                 )
-            if k < 3:
-                residual[k] = keep.tile([P, PACK, P], F32, name="residual%d" % k, tag="chain%d" % (k - 1), align_bytes=64)
-                nc.vector.tensor_tensor(residual[k][:], rec[:], target[c, b], ALU.subtract)
-            else:
-                staged = keep.tile([P, PACK, P], F32, name="staged%d" % k, tag="grad%d" % (k - 1), align_bytes=64)
-                nc.scalar.copy(staged[:], rec[:])
-                residual[k] = keep.tile([P, PACK, P], F32, name="residual%d" % k, tag="chain%d" % (k - 1), align_bytes=64)
-                nc.gpsimd.tensor_tensor(residual[k][:], staged[:], target[c, b], ALU.subtract)
+            residual[k] = keep.tile([P, PACK, P], F32, name="residual%d" % k, tag="chain%d" % (k - 1), align_bytes=64)
+            nc.vector.tensor_tensor(residual[k][:], rec[:], target[c, b], ALU.subtract)
 
         def clip(k):
-            clipped[k] = keep.tile([P, P, PACK], F32, name="clipped%d" % k, tag="chain%d" % k, align_bytes=64)
-            nc.vector.tensor_scalar(
-                clipped[k][:].rearrange("p (c i) t -> p c t i", i=4),
-                residual[k][:].rearrange("p t (c i) -> p c t i", i=4),
-                -1.0,
-                1.0,
-                ALU.max,
-                ALU.min,
-            )
+            if k < EARLY:
+                clipped[k] = keep.tile([P, P, PACK], F32, name="clipped%d" % k, tag="chain%d" % k, align_bytes=64)
+                nc.vector.tensor_scalar(
+                    clipped[k][:].rearrange("p (c i) t -> p c t i", i=4),
+                    residual[k][:].rearrange("p t (c i) -> p c t i", i=4),
+                    -1.0,
+                    1.0,
+                    ALU.max,
+                    ALU.min,
+                )
+            else:
+                clipped[k] = keep.tile([P, PACK, P], F32, name="clipped%d" % k, tag="clipped%d" % k, align_bytes=64)
+                nc.vector.tensor_scalar(clipped[k][:], residual[k][:], -1.0, 1.0, ALU.max, ALU.min)
 
         def weigh(k):
             c, b = units[k]
             grouped = keep.tile([P, P * PACK], BF16, name="e_grouped%d" % k, tag=("grad%d" % (k - 2) if k >= 2 else "e_first%d" % k), align_bytes=64)
-            (nc.vector if k == 0 else nc.gpsimd).tensor_tensor(
-                grouped[:].rearrange("p (d t) -> p d t", t=PACK),
-                clipped[k][:],
-                weight[:, b : b + 1, :].to_broadcast([P, P, PACK]),
-                ALU.mult,
-            )
+            if k < EARLY:
+                nc.vector.tensor_tensor(
+                    grouped[:].rearrange("p (d t) -> p d t", t=PACK),
+                    clipped[k][:],
+                    weight[:, b : b + 1, :].to_broadcast([P, P, PACK]),
+                    ALU.mult,
+                )
+            else:
+                rows = keep.tile([P, PACK, P], BF16, name="e_rows%d" % k, tag="chain%d" % k, align_bytes=64)
+                for t in range(PACK):
+                    nc.scalar.activation(rows[:, t, :], clipped[k][:, t, :], COPY, scale=weight[:, b, t : t + 1])
+                nc.scalar.copy(
+                    grouped[:].rearrange("p (c i t) -> p c t i", i=4, t=PACK),
+                    rows[:].rearrange("p t (c i) -> p c t i", i=4),
+                )
             e_grouped[k] = grouped
 
         def differentiate(k):
@@ -212,6 +221,13 @@ def tile_attend_gdi_hub_w_kernel(tc, zT, wT, xm, wt, zm, offs, out):
 
         def scatter(k, h):
             c, b = units[k]
+            if k == len(units) - 1:
+                if h == 0:
+                    whole = keep.tile([P, N], F32, name="grad_last")
+                    nc.scalar.copy(whole[:], banks[k][:])
+                    nc.vector.tensor_copy(listed(window[c % 3], b), whole[:])
+                    nc.sync.dma_start(out[c * P : (c + 1) * P, :], window[c % 3][:])
+                return
             tag = "grad%d" % k
             if h == 1 and k == 0:
                 tag = "target01"
@@ -246,34 +262,35 @@ def tile_attend_gdi_hub_w_kernel(tc, zT, wT, xm, wt, zm, offs, out):
         gather(3)
         rebuild(1)
         clip(1)
-        scatter(0, 1)
         prepare_zT(1, ("scalar", "scalar"))
         weigh(1)
-        rebuild(2)
         differentiate(1)
+        scatter(0, 1)
+        rebuild(2)
         clip(2)
-        gather(4)
         prepare_zm(1, ("scalar", "scalar"))
         turn(3)
-        turn(4)
-        gather(5)
         scatter(1, 0)
+        cast_table(2, 0, "scalar")
+        cast_table(2, 1, "scalar")
+        gather(4)
         weigh(2)
-        rebuild(3)
-        cast_table(3, 0)
         for k in range(1, len(units)):
+            if k + 2 < len(units):
+                rebuild(k + 2)
             if k + 1 < len(units):
                 differentiate(k + 1)
-            if k + 4 < len(units):
-                turn(k + 4)
             if k + 2 < len(units):
                 clip(k + 2)
             scatter(k, 1)
+            if k + 3 < len(units):
+                turn(k + 3)
+            if k == 1:
+                cast_table(3, 0, "scalar")
+                cast_table(3, 1, "vector")
             if k + 1 < len(units):
                 scatter(k + 1, 0)
             if k + 2 < len(units):
                 weigh(k + 2)
-            if k + 3 < len(units):
-                rebuild(k + 3)
-            if k + 5 < len(units):
-                gather(k + 5)
+            if k + 4 < len(units):
+                gather(k + 4)

@@ -127,16 +127,15 @@ def tile_attend_gdi_hub_w_kernel(tc, zT, wT, xm, wt, zm, offs, out):
         def listed(tile, b, lo=0, hi=COLS):
             return tile[:].indirect(offsets[:, b * COLS + lo : b * COLS + hi])
 
-        def cast_table(c, h, engine):
-            if c not in table16:
-                table16[c] = keep.tile([P, T], BF16, name="table16_%d" % c, tag=("picked4" if c == 3 else "zm_raw11"), align_bytes=64)
-            cols = slice(h * T // 2, (h + 1) * T // 2)
-            cast(engine, table16[c][:, cols], table[c][:, cols])
+        def cast_table(c, lo, hi):
+            if lo == 0:
+                table16[c] = keep.tile([P, T], BF16, name="table16_%d" % c, tag=("e1_codes" if c == 3 else "zm_raw11"), align_bytes=64)
+            cast("scalar", table16[c][:, lo:hi], table[c][:, lo:hi])
 
         def gather(k):
             c, b = units[k]
-            picked[k] = keep.tile([P, N], BF16, name="picked%d" % k, tag=("clipped%d" % (k - 2) if k >= 5 else ["picked0", "e_first0", "picked2", "e0_codes", "picked4"][k]), align_bytes=64)
-            if c < 2:
+            picked[k] = keep.tile([P, N], BF16, name="picked%d" % k, tag=("clipped%d" % (k - 2) if k >= 5 else ["picked0", "e_first0", "picked2", "e0_codes", "e1_codes"][k]), align_bytes=64)
+            if k < 5:
                 nc.vector.tensor_copy(picked[k][:], listed(table[c], b))
             else:
                 nc.scalar.activation(picked[k][:], listed(table16[c], b), COPY)
@@ -189,7 +188,7 @@ def tile_attend_gdi_hub_w_kernel(tc, zT, wT, xm, wt, zm, offs, out):
             c, b = units[k]
             grouped = keep.tile([P, P * PACK], BF16, name="e_grouped%d" % k, tag=("grad%d" % (k - 2) if k >= 2 else "e_first%d" % k), align_bytes=64)
             if k < EARLY:
-                nc.vector.tensor_tensor(
+                (nc.vector if k == 0 else nc.gpsimd).tensor_tensor(
                     grouped[:].rearrange("p (d t) -> p d t", t=PACK),
                     clipped[k][:],
                     weight[:, b : b + 1, :].to_broadcast([P, P, PACK]),
@@ -262,18 +261,20 @@ def tile_attend_gdi_hub_w_kernel(tc, zT, wT, xm, wt, zm, offs, out):
         gather(3)
         rebuild(1)
         clip(1)
+        scatter(0, 1)
         prepare_zT(1, ("scalar", "scalar"))
         weigh(1)
-        differentiate(1)
-        scatter(0, 1)
         rebuild(2)
+        differentiate(1)
         clip(2)
+        gather(4)
         prepare_zm(1, ("scalar", "scalar"))
         turn(3)
+        cast_table(2, 0, T // 2)
         scatter(1, 0)
-        cast_table(2, 0, "scalar")
-        cast_table(2, 1, "scalar")
-        gather(4)
+        cast_table(2, T // 2, T)
+        turn(4)
+        cast_table(3, 0, T)
         weigh(2)
         for k in range(1, len(units)):
             if k + 2 < len(units):
@@ -283,11 +284,8 @@ def tile_attend_gdi_hub_w_kernel(tc, zT, wT, xm, wt, zm, offs, out):
             if k + 2 < len(units):
                 clip(k + 2)
             scatter(k, 1)
-            if k + 3 < len(units):
+            if k > 1 and k + 3 < len(units):
                 turn(k + 3)
-            if k == 1:
-                cast_table(3, 0, "scalar")
-                cast_table(3, 1, "vector")
             if k + 1 < len(units):
                 scatter(k + 1, 0)
             if k + 2 < len(units):

from contextlib import ExitStack

import concourse.mybir as mybir
from concourse.masks import make_identity

B, N, T, D, R = 2, 512, 2048, 512, 512
FLOPS = 2 * 2 * B * N * D * R

F32 = mybir.dt.float32
BF16 = mybir.dt.bfloat16
U32 = mybir.dt.uint32
U16 = mybir.dt.uint16
U8 = mybir.dt.uint8
E4M3 = mybir.dt.float8_e4m3fn_x4
E5M2 = mybir.dt.float8_e5m2_x4
ALU = mybir.AluOpType
COPY = mybir.ActivationFunctionType.Copy

P = 128
PACK = 4
HALF = 256
COLS = N // 16
EARLY = 3


def tile_attend_gdi_hub_w_kernel(tc, zT, wT, xm, wt, zm, offs, out):
    nc = tc.nc
    with ExitStack() as ctx:
        keep = ctx.enter_context(tc.tile_pool(name="keep", bufs=1))
        work = ctx.enter_context(tc.tile_pool(name="work", bufs=2))
        turn_psum = ctx.enter_context(tc.psum_pool(name="turn_psum", bufs=2))
        rec_psum = ctx.enter_context(tc.psum_pool(name="rec_psum", bufs=3))
        grad_psum = ctx.enter_context(tc.psum_pool(name="grad_psum", bufs=3))

        offsets = keep.tile([P, B * COLS], U16, name="offsets")

        table = {}
        zT_raw = {}
        zm_raw = {}
        target = {}

        def load_table(c):
            table[c] = keep.tile([P, T], F32, name="table%d" % c, tag="table%d" % c, align_bytes=64)
            nc.sync.dma_start(table[c][:], wT[c * P : (c + 1) * P, :])

        def load_rows(src, raw, name, b):
            for h in range(2):
                raw[b, h] = keep.tile([P, PACK, HALF], F32, name="%s%d%d" % (name, b, h), tag="%s%d%d" % (name, b, h), align_bytes=64)
                nc.sync.dma_start(
                    raw[b, h][:], src[b].rearrange("(p j) w -> p j w", j=PACK)[:, :, h * HALF : (h + 1) * HALF]
                )

        def load_target(b, c0, c1):
            t = keep.tile([P, PACK, (c1 - c0) * P], F32, name="target%d%d" % (b, c0), tag="target%d%d" % (b, c0), align_bytes=64)
            nc.sync.dma_start(t[:], xm[b].rearrange("(p t) d -> p t d", t=PACK)[:, :, c0 * P : c1 * P])
            for c in range(c0, c1):
                target[c, b] = t[:, :, (c - c0) * P : (c - c0 + 1) * P]

        load_table(0)
        nc.sync.dma_start(offsets[:], offs)
        load_rows(zT, zT_raw, "zT_raw", 0)
        weight = keep.tile([P, B, PACK], F32, name="weight")
        nc.sync.dma_start(weight[:], wt.rearrange("b (p t) o -> p b (t o)", t=PACK))
        load_target(0, 0, 1)
        load_rows(zm, zm_raw, "zm_raw", 0)
        load_table(1)
        load_target(0, 1, 2)
        load_rows(zT, zT_raw, "zT_raw", 1)
        load_target(1, 0, 1)
        load_rows(zm, zm_raw, "zm_raw", 1)
        load_table(2)
        load_target(1, 1, 2)
        load_target(0, 2, 3)
        load_table(3)
        load_target(1, 2, 3)
        load_target(0, 3, 4)
        load_target(1, 3, 4)

        identity = keep.tile([P, P], F32, name="identity")
        make_identity(nc, identity[:])

        window = []
        for c in range(3):
            w = keep.tile([P, T], F32, name="window%d" % c)
            (nc.vector if c < 2 else nc.gpsimd).memset(w[:], 0.0)
            window.append(w)

        def cast(engine, out_ap, in_ap):
            if engine == "vector":
                nc.vector.tensor_copy(out_ap, in_ap)
            else:
                nc.scalar.activation(out_ap, in_ap, COPY)

        def quantize(name, grouped, words, fmt):
            codes = keep.tile([P, words], U32, name=name + "_codes", tag=name + "_codes", align_bytes=64)
            scales = keep.tile([P, words], U8, name=name + "_scales", align_bytes=64)
            nc.vector.quantize_mx(out=codes[:].bitcast(fmt), scales=scales[:], in_=grouped)
            return codes, scales

        zT_q = {}
        zm_q = {}

        def prepare_zT(b, engines):
            grouped = keep.tile([P, R * PACK], BF16, name="zT_grouped%d" % b, tag=["zT_grouped", "e_first0"][b], align_bytes=64)
            view = grouped[:].rearrange("p (t m j) -> p m j t", t=PACK, j=PACK)
            for h in range(2):
                cast(engines[h], view[:, h * 64 : (h + 1) * 64], zT_raw[b, h][:].rearrange("p j (m t) -> p m j t", t=PACK))
            zT_q[b] = quantize("zT%d" % b, grouped[:], R, E4M3)

        def prepare_zm(b, engines):
            grouped = keep.tile([P, N * PACK], BF16, name="zm_grouped%d" % b, tag=["picked2", "zT_raw11"][b], align_bytes=64)
            view = grouped[:].rearrange("p (c i j) -> p c j i", i=4, j=PACK)
            for h in range(2):
                cast(engines[h], view[:, h * 64 : (h + 1) * 64], zm_raw[b, h][:].rearrange("p j (c i) -> p c j i", i=4))
            zm_q[b] = quantize("zm%d" % b, grouped[:], N, E4M3)

        units = [(0, 0), (1, 0), (0, 1), (1, 1), (2, 0), (2, 1), (3, 0), (3, 1)]
        table16 = {}
        picked = {}
        atoms_q = {}
        clipped = {}
        e_q = {}
        e_grouped = {}
        residual = {}
        banks = {}

        def listed(tile, b, lo=0, hi=COLS):
            return tile[:].indirect(offsets[:, b * COLS + lo : b * COLS + hi])

        def cast_table(c, lo, hi):
            if lo == 0:
                table16[c] = keep.tile([P, T], BF16, name="table16_%d" % c, tag=("e1_codes" if c == 3 else "zm_raw11"), align_bytes=64)
            cast("scalar", table16[c][:, lo:hi], table[c][:, lo:hi])

        def gather(k):
            c, b = units[k]
            picked[k] = keep.tile([P, N], BF16, name="picked%d" % k, tag=("clipped%d" % (k - 2) if k >= 5 else ["picked0", "e_first0", "picked2", "e0_codes", "e1_codes"][k]), align_bytes=64)
            if k < 5:
                nc.vector.tensor_copy(picked[k][:], listed(table[c], b))
            else:
                nc.scalar.activation(picked[k][:], listed(table16[c], b), COPY)

        def turn(k):
            words = picked[k][:].bitcast(F32)
            turned = turn_psum.tile([P, 2, P], F32, name="turned")
            for u in range(2):
                nc.tensor.transpose(turned[:, u, :], words[:, u : 2 * P : 2], identity[:])
            grouped = keep.tile([P, P * PACK], BF16, name="atoms_grouped%d" % k, tag=("atoms%d" % k if k >= 4 else ["zT_raw00", "e0_codes", "atoms2", "zm_raw10"][k]), align_bytes=64)
            nc.scalar.copy(
                grouped[:].bitcast(F32).rearrange("p (d u) -> p d u", u=2), turned[:].rearrange("p u d -> p d u")
            )
            atoms_q[k] = quantize("atoms%d" % k, grouped[:], P, E4M3)

        def rebuild(k):
            c, b = units[k]
            rec = rec_psum.tile([P, PACK, P], F32, name="rec")
            z_codes, z_scales = zT_q[b]
            a_codes, a_scales = atoms_q[k]
            for t in range(PACK):
                nc.tensor.matmul_mx(
                    out=rec[:, t, :],
                    lhsT=z_codes[:, t * P : (t + 1) * P].bitcast(E4M3),
                    lhsT_scale=z_scales[:, t * P : (t + 1) * P],
                    rhs=a_codes[:].bitcast(E4M3),
                    rhs_scale=a_scales[:],
                    start=True,
                    stop=True,
                )
            residual[k] = keep.tile([P, PACK, P], F32, name="residual%d" % k, tag="chain%d" % (k - 1), align_bytes=64)
            nc.vector.tensor_tensor(residual[k][:], rec[:], target[c, b], ALU.subtract)

        def clip(k):
            if k < EARLY:
                clipped[k] = keep.tile([P, P, PACK], F32, name="clipped%d" % k, tag="chain%d" % k, align_bytes=64)
                nc.vector.tensor_scalar(
                    clipped[k][:].rearrange("p (c i) t -> p c t i", i=4),
                    residual[k][:].rearrange("p t (c i) -> p c t i", i=4),
                    -1.0,
                    1.0,
                    ALU.max,
                    ALU.min,
                )
            else:
                clipped[k] = keep.tile([P, PACK, P], F32, name="clipped%d" % k, tag="clipped%d" % k, align_bytes=64)
                nc.vector.tensor_scalar(clipped[k][:], residual[k][:], -1.0, 1.0, ALU.max, ALU.min)

        def weigh(k):
            c, b = units[k]
            grouped = keep.tile([P, P * PACK], BF16, name="e_grouped%d" % k, tag=("grad%d" % (k - 2) if k >= 2 else "e_first%d" % k), align_bytes=64)
            if k < EARLY:
                (nc.vector if k == 0 else nc.gpsimd).tensor_tensor(
                    grouped[:].rearrange("p (d t) -> p d t", t=PACK),
                    clipped[k][:],
                    weight[:, b : b + 1, :].to_broadcast([P, P, PACK]),
                    ALU.mult,
                )
            else:
                rows = keep.tile([P, PACK, P], BF16, name="e_rows%d" % k, tag="chain%d" % k, align_bytes=64)
                for t in range(PACK):
                    nc.scalar.activation(rows[:, t, :], clipped[k][:, t, :], COPY, scale=weight[:, b, t : t + 1])
                nc.scalar.copy(
                    grouped[:].rearrange("p (c i t) -> p c t i", i=4, t=PACK),
                    rows[:].rearrange("p t (c i) -> p c t i", i=4),
                )
            e_grouped[k] = grouped

        def differentiate(k):
            c, b = units[k]
            e_q[k] = quantize("e%d" % k, e_grouped[k][:], P, E5M2)
            banks[k] = grad_psum.tile([P, N], F32, name="grad_bank")
            nc.tensor.matmul_mx(
                out=banks[k][:],
                lhsT=e_q[k][0][:].bitcast(E5M2),
                lhsT_scale=e_q[k][1][:],
                rhs=zm_q[b][0][:].bitcast(E4M3),
                rhs_scale=zm_q[b][1][:],
                start=True,
                stop=True,
            )

        def scatter(k, h):
            c, b = units[k]
            if k == len(units) - 1:
                if h == 0:
                    whole = keep.tile([P, N], F32, name="grad_last")
                    nc.scalar.copy(whole[:], banks[k][:])
                    nc.vector.tensor_copy(listed(window[c % 3], b), whole[:])
                    nc.sync.dma_start(out[c * P : (c + 1) * P, :], window[c % 3][:])
                return
            tag = "grad%d" % k
            if h == 1 and k == 0:
                tag = "target01"
            elif h == 1 and k + 2 < len(units):
                tag = "target%d%d" % (units[k + 2][1], units[k + 2][0])
            elif h == 1 and k + 1 < len(units):
                tag = "chain%d" % (k + 1)
            elif h == 1:
                tag = "last"
            part = keep.tile([P, HALF], F32, name="grad%d%d" % (k, h), tag=tag, align_bytes=64)
            if (k, h) == (0, 1):
                nc.vector.tensor_copy(part[:], banks[k][:, h * HALF : (h + 1) * HALF])
            else:
                nc.scalar.copy(part[:], banks[k][:, h * HALF : (h + 1) * HALF])
            nc.vector.tensor_copy(listed(window[c % 3], b, h * COLS // 2, (h + 1) * COLS // 2), part[:])
            if b == B - 1 and h == 1:
                nc.sync.dma_start(out[c * P : (c + 1) * P, :], window[c % 3][:])

        gather(0)
        prepare_zT(0, ("scalar", "vector"))
        turn(0)
        rebuild(0)
        gather(2)
        turn(2)
        clip(0)
        prepare_zm(0, ("scalar", "scalar"))
        weigh(0)
        differentiate(0)
        gather(1)
        scatter(0, 0)
        turn(1)
        gather(3)
        rebuild(1)
        clip(1)
        scatter(0, 1)
        prepare_zT(1, ("scalar", "scalar"))
        weigh(1)
        rebuild(2)
        differentiate(1)
        clip(2)
        gather(4)
        prepare_zm(1, ("scalar", "scalar"))
        turn(3)
        cast_table(2, 0, T // 2)
        scatter(1, 0)
        cast_table(2, T // 2, T)
        turn(4)
        cast_table(3, 0, T)
        weigh(2)
        for k in range(1, len(units)):
            if k + 2 < len(units):
                rebuild(k + 2)
            if k + 1 < len(units):
                differentiate(k + 1)
            if k + 2 < len(units):
                clip(k + 2)
            scatter(k, 1)
            if k > 1 and k + 3 < len(units):
                turn(k + 3)
            if k + 1 < len(units):
                scatter(k + 1, 0)
            if k + 2 < len(units):
                weigh(k + 2)
            if k + 4 < len(units):
                gather(k + 4)
